import numpy as np
import ml_dtypes


def mxq(x, axis, fmt="e4m3"):
    dtype, down = {"e4m3": (ml_dtypes.float8_e4m3fn, 7), "e5m2": (ml_dtypes.float8_e5m2, 14)}[fmt]
    v = np.moveaxis(np.asarray(x, np.float32).astype(ml_dtypes.bfloat16).astype(np.float64), axis, -1)
    blocks = v.reshape(v.shape[:-1] + (-1, 32))
    amax = np.abs(blocks).max(-1, keepdims=True)
    byte = np.maximum(np.where(amax > 0, np.frexp(amax)[1] - 1 + 127, 0) - down, 1)
    scale = np.exp2(byte - 127.0)
    codes = (blocks / scale).astype(np.float32).astype(dtype).astype(np.float64)
    return np.moveaxis((codes * scale).reshape(v.shape), -1, axis)


WIDE = False


def mx_kscale(k):
    if not WIDE:
        return np.ones(k)
    levels = np.array([10, -10, 5, -5, 0])
    if k % 512:
        return np.exp2(np.random.permutation(np.resize(levels, k // 32))).repeat(32)
    a = np.empty((k // 512, 16))
    for p in range(k // 512):
        a[p, :8] = np.random.permutation(np.resize(levels, 8))
        for g in range(8):
            far = levels[np.abs(levels - a[p, g]) >= 10]
            a[p, g + 8] = far[np.random.randint(len(far))]
    return np.exp2(a.ravel()).repeat(32)


def f64(x):
    return np.asarray(x).astype(np.float64)


def striped8(idx):
    return np.asarray(idx).reshape(8, -1, 16).transpose(0, 2, 1).reshape(128, -1).astype(np.uint16)


def unstriped8(offs):
    return offs.reshape(8, 16, -1).transpose(0, 2, 1).reshape(8, -1).astype(np.int64)


def pick8(x, idx, run):
    r = np.arange(len(x))
    return x[r[:, None], idx[r % (8 * run) // run]]


E2M1 = np.array([0.0, 0.5, 1.0, 1.5, 2.0, 3.0, 4.0, 6.0, -0.0, -0.5, -1.0, -1.5, -2.0, -3.0, -4.0, -6.0])


def pack_weight(w, fmt):
    k, n = w.shape
    w = f64(np.asarray(w, np.float32).astype(ml_dtypes.bfloat16)).reshape(k // 32, 32, n)
    amax = np.abs(w).max(1)
    if fmt == "e4m3":
        byte = np.frexp(amax)[1] - 1 + 127 - 7
    else:
        mant, ex = np.frexp(amax / 6.0)
        byte = np.where(mant > 0.5, ex, ex - 1) + 127
    byte = np.clip(np.where(amax > 0, byte, 1), 1, 254)
    scaled = (w * np.exp2(127.0 - byte)[:, None, :]).reshape(k, n).astype(np.float32)
    by_word = np.ascontiguousarray(scaled.reshape(k // 512, 128, 4, n).transpose(0, 1, 3, 2))
    if fmt == "e4m3":
        words = by_word.astype(ml_dtypes.float8_e4m3fn).view(np.uint8)
    else:
        c = by_word.astype(ml_dtypes.float4_e2m1fn).view(np.uint8) & 0xF
        words = (c[..., 0::2] | (c[..., 1::2] << 4)).reshape(k // 512, 128, 2 * n)
    return np.ascontiguousarray(words), np.ascontiguousarray(byte.astype(np.uint8).reshape(k // 512, 16, n))


def unpack_weight(words, scales, fmt):
    g, _, n = scales.shape
    words = np.ascontiguousarray(words).reshape(g, 128, n, -1)
    if fmt == "e4m3":
        vals = words.view(ml_dtypes.float8_e4m3fn).astype(np.float64)
    else:
        nib = np.empty((g, 128, n, 4), np.uint8)
        nib[..., 0::2] = words & 0xF
        nib[..., 1::2] = words >> 4
        vals = E2M1[nib]
    vals = vals * np.repeat(np.exp2(scales.astype(np.float64) - 127.0), 8, axis=1)[..., None]
    return vals.transpose(0, 1, 3, 2).reshape(g * 512, n)


def sgn(shape):
    return np.random.uniform(0.5, 2.0, shape) * np.where(np.random.standard_normal(shape) < 0, -1.0, 1.0)


D, T, U, X, I, Q = 512, 1024, 1024, 1024, 512, 128


def setup_inputs():
    n = np.random.standard_normal
    idx = np.stack([np.random.permutation(T)[:I] for _ in range(8)])
    idx2 = np.stack([np.random.permutation(U)[:I] for _ in range(8)])
    idx3 = np.stack([np.random.permutation(U)[:I] for _ in range(8)])
    idx4 = np.stack([np.random.permutation(X)[:I] for _ in range(8)])
    idx5 = np.stack([np.random.permutation(X)[:I] for _ in range(8)])
    fd = mx_kscale(D)
    cachep = pack_weight(n((D, T)) / fd[:, None], "e4m3")
    draftp = pack_weight(n((D, U)) / fd[:, None], "e2m1")
    archp = pack_weight(n((D, X)) / fd[:, None], "e4m3")
    return {
        "query": (n((D, Q)) * 1.0 / np.sqrt(D) * fd[:, None]).astype(np.float32),
        "cache_words": cachep[0],
        "cache_scales": cachep[1],
        "draft_words": draftp[0],
        "draft_scales": draftp[1],
        "arch_words": archp[0],
        "arch_scales": archp[1],
        "sa": (sgn((Q, 1))).astype(np.float32),
        "sb": (sgn((Q, 1))).astype(np.float32),
        "offs": striped8(idx),
        "offs2": striped8(idx2),
        "offs3": striped8(idx3),
        "offs4": striped8(idx4),
        "offs5": striped8(idx5),
    }


def reference(query, cache_words, cache_scales, draft_words, draft_scales, arch_words, arch_scales, sa, sb, offs, offs2, offs3, offs4, offs5):
    idx = unstriped8(offs)
    idx2 = unstriped8(offs2)
    idx3 = unstriped8(offs3)
    idx4 = unstriped8(offs4)
    idx5 = unstriped8(offs5)
    cacheu = unpack_weight(cache_words, cache_scales, "e4m3")
    draftu = unpack_weight(draft_words, draft_scales, "e2m1")
    archu = unpack_weight(arch_words, arch_scales, "e4m3")
    queryq = mxq(f64(query), 0, "e4m3")
    a = queryq.T @ cacheu
    b = queryq.T @ draftu
    c0 = queryq.T @ archu
    w = pick8(a, idx, 16) * f64(sa)
    f1 = np.zeros((Q, U))
    f1[np.arange(Q)[:, None], idx2[np.arange(Q) % 128 // 16]] = w
    bb = b - f1
    v = pick8(bb, idx3, 16) * f64(sb)
    f2 = np.zeros((Q, X))
    f2[np.arange(Q)[:, None], idx4[np.arange(Q) % 128 // 16]] = v
    cc = np.maximum(c0, f2)
    y = pick8(cc, idx5, 16)
    return y

@@ -1,0 +1,134 @@
+from contextlib import ExitStack
+
+import concourse.mybir as mybir
+
+F32 = mybir.dt.float32
+BF16 = mybir.dt.bfloat16
+I32 = mybir.dt.int32
+U32 = mybir.dt.uint32
+U16 = mybir.dt.uint16
+U8 = mybir.dt.uint8
+FP8X4 = mybir.dt.float8_e4m3fn_x4
+FP4X4 = mybir.dt.float4_e2m1fn_x4
+COPY = mybir.ActivationFunctionType.Copy
+SUBTRACT = mybir.AluOpType.subtract
+MAX = mybir.AluOpType.max
+
+P = 128
+PACK = 4
+TOKENS = 1024
+SLOTS = 512
+BANK = 512
+LIST_COLS = SLOTS // 16
+FLOPS = 3 * 2 * 512 * P * TOKENS
+
+
+def load_scale_rows(nc, plane, scales):
+    rows = scales[0].bitcast(I32)
+    for quad in range(4):
+        nc.sync.dma_start(out=plane[32 * quad : 32 * quad + 4, :].bitcast(I32), in_=rows[4 * quad : 4 * quad + 4, :])
+
+
+def load_list(nc, pool, offs, name):
+    tile = pool.tile([P, LIST_COLS], U16, name=name)
+    nc.sync.dma_start(tile[:], offs)
+    return tile
+
+
+def tile_attend_scaledhops_three_kernel(
+    tc, query, cache_words, cache_scales, draft_words, draft_scales, arch_words, arch_scales,
+    sa, sb, offs, offs2, offs3, offs4, offs5, out,
+):
+    nc = tc.nc
+    with ExitStack() as ctx:
+        sbuf = ctx.enter_context(tc.tile_pool(name="sbuf", bufs=1))
+        psum = ctx.enter_context(tc.psum_pool(name="psum", bufs=1))
+
+        cache_plane = sbuf.tile([P, TOKENS], U8, align_bytes=64)
+        draft_plane = sbuf.tile([P, TOKENS], U8, align_bytes=64)
+        arch_plane = sbuf.tile([P, TOKENS], U8, align_bytes=64)
+        f1 = sbuf.tile([P, TOKENS], F32)
+        f2 = sbuf.tile([P, TOKENS], F32)
+        nc.vector.memset(cache_plane[:].bitcast(I32), 0)
+        nc.vector.memset(draft_plane[:].bitcast(I32), 0)
+        nc.vector.memset(arch_plane[:].bitcast(I32), 0)
+        nc.vector.memset(f1[:], 0.0)
+        nc.vector.memset(f2[:], 0.0)
+
+        q_raw = sbuf.tile([P, PACK, P], F32)
+        nc.sync.dma_start(out=q_raw[:], in_=query.rearrange("(p j) q -> p j q", j=PACK))
+        load_scale_rows(nc, cache_plane, cache_scales)
+        cache_rows = cache_words[0].rearrange("p n t -> p (n t)").bitcast(I32)
+        cache_halves = []
+        for half in range(2):
+            words = sbuf.tile([P, BANK], U32, name="cache%d" % half, align_bytes=64)
+            nc.sync.dma_start(out=words[:].bitcast(I32), in_=cache_rows[:, half * BANK : (half + 1) * BANK])
+            cache_halves.append(words)
+        idx = load_list(nc, sbuf, offs, "idx")
+        sa_col = sbuf.tile([P, 1], F32)
+        nc.sync.dma_start(out=sa_col[:], in_=sa)
+        idx2 = load_list(nc, sbuf, offs2, "idx2")
+        load_scale_rows(nc, draft_plane, draft_scales)
+        draft = sbuf.tile([P, 2 * TOKENS], U8, align_bytes=64)
+        nc.sync.dma_start(out=draft[:].bitcast(I32), in_=draft_words[0].bitcast(I32))
+        idx3 = load_list(nc, sbuf, offs3, "idx3")
+        sb_col = sbuf.tile([P, 1], F32)
+        nc.sync.dma_start(out=sb_col[:], in_=sb)
+        idx4 = load_list(nc, sbuf, offs4, "idx4")
+        load_scale_rows(nc, arch_plane, arch_scales)
+        arch = sbuf.tile([P, TOKENS], U32, align_bytes=64)
+        nc.sync.dma_start(out=arch[:].bitcast(I32), in_=arch_words[0].rearrange("p n t -> p (n t)").bitcast(I32))
+        idx5 = load_list(nc, sbuf, offs5, "idx5")
+
+        q_bf = sbuf.tile([P, P, PACK], BF16, align_bytes=64)
+        nc.vector.tensor_copy(out=q_bf[:], in_=q_raw[:].rearrange("p j q -> p q j"))
+        q_words = sbuf.tile([P, P], U32, align_bytes=64)
+        q_plane = sbuf.tile([P, P], U8, align_bytes=64)
+        nc.vector.quantize_mx(out=q_words[:].bitcast(FP8X4), scales=q_plane[:], in_=q_bf[:].rearrange("p q j -> p (q j)"))
+
+        def score(name, rhs, rhs_scale, width):
+            bank = psum.tile([P, width], F32, name=name)
+            nc.tensor.matmul_mx(
+                out=bank[:], lhsT=q_words[:].bitcast(FP8X4), lhsT_scale=q_plane[:],
+                rhs=rhs, rhs_scale=rhs_scale, start=True, stop=True,
+            )
+            return bank
+
+        a = sbuf.tile([P, TOKENS], F32)
+        piece = 256
+        for k in range(TOKENS // piece):
+            lo = k * piece
+            words = cache_halves[lo // BANK]
+            bank = score("a%d" % k, words[:, lo % BANK : lo % BANK + piece].bitcast(FP8X4), cache_plane[:, lo : lo + piece], piece)
+            if k % 2 == 0:
+                nc.vector.tensor_copy(out=a[:, lo : lo + piece], in_=bank[:])
+            else:
+                nc.scalar.activation(out=a[:, lo : lo + piece], in_=bank[:], func=COPY)
+
+        w = sbuf.tile([P, SLOTS], F32)
+        nc.scalar.activation(out=w[:], in_=a[:].indirect(idx[:]), func=COPY, scale=sa_col[:])
+        nc.scalar.activation(out=f1[:].indirect(idx2[:]), in_=w[:], func=COPY)
+
+        bb = sbuf.tile([P, TOKENS], F32)
+        for half in range(2):
+            cols = slice(half * BANK, (half + 1) * BANK)
+            bank = score("b%d" % half, draft[:, 2 * half * BANK : 2 * (half + 1) * BANK].bitcast(FP4X4), draft_plane[:, cols], BANK)
+            nc.vector.tensor_tensor(out=bb[:, cols], in0=bank[:], in1=f1[:, cols], op=SUBTRACT)
+
+        v = sbuf.tile([P, SLOTS], F32)
+        nc.scalar.activation(out=v[:], in_=bb[:].indirect(idx3[:]), func=COPY, scale=sb_col[:])
+        nc.scalar.activation(out=f2[:].indirect(idx4[:]), in_=v[:], func=COPY)
+
+        cc = sbuf.tile([P, TOKENS], F32)
+        for half in range(2):
+            cols = slice(half * BANK, (half + 1) * BANK)
+            bank = score("c%d" % half, arch[:, cols].bitcast(FP8X4), arch_plane[:, cols], BANK)
+            nc.vector.tensor_tensor(out=cc[:, cols], in0=bank[:], in1=f2[:, cols], op=MAX)
+
+        share = SLOTS // 2
+        y0 = sbuf.tile([P, share], F32)
+        y1 = sbuf.tile([P, share], F32)
+        nc.vector.tensor_copy(out=y0[:], in_=cc[:].indirect(idx5[:, : LIST_COLS // 2]))
+        nc.scalar.activation(out=y1[:], in_=cc[:].indirect(idx5[:, LIST_COLS // 2 :]), func=COPY)
+        nc.sync.dma_start(out=out[:, :share], in_=y0[:])
+        nc.scalar.dma_start(out=out[:, share:], in_=y1[:])

@@ -47,13 +47,11 @@ def tile_attend_scaledhops_three_kernel(
         cache_plane = sbuf.tile([P, TOKENS], U8, align_bytes=64)
         draft_plane = sbuf.tile([P, TOKENS], U8, align_bytes=64)
         arch_plane = sbuf.tile([P, TOKENS], U8, align_bytes=64)
-        f1 = sbuf.tile([P, TOKENS], F32)
-        f2 = sbuf.tile([P, TOKENS], F32)
+        f1a = sbuf.tile([P, TOKENS], F32, tag="a_then_f2")
         nc.vector.memset(cache_plane[:].bitcast(I32), 0)
         nc.vector.memset(draft_plane[:].bitcast(I32), 0)
         nc.vector.memset(arch_plane[:].bitcast(I32), 0)
-        nc.vector.memset(f1[:], 0.0)
-        nc.vector.memset(f2[:], 0.0)
+        nc.vector.memset(f1a[:], 0.0)
 
         q_raw = sbuf.tile([P, PACK, P], F32)
         nc.sync.dma_start(out=q_raw[:], in_=query.rearrange("(p j) q -> p j q", j=PACK))
@@ -80,14 +78,25 @@ def tile_attend_scaledhops_three_kernel(
         nc.sync.dma_start(out=arch[:].bitcast(I32), in_=arch_words[0].rearrange("p n t -> p (n t)").bitcast(I32))
         idx5 = load_list(nc, sbuf, offs5, "idx5")
 
-        q_bf = sbuf.tile([P, P, PACK], BF16, align_bytes=64)
-        nc.vector.tensor_copy(out=q_bf[:], in_=q_raw[:].rearrange("p j q -> p q j"))
+        q_bf = sbuf.tile([P, P, PACK], BF16, tag="q_bf_then_f1b", align_bytes=64)
         q_words = sbuf.tile([P, P], U32, align_bytes=64)
         q_plane = sbuf.tile([P, P], U8, align_bytes=64)
-        nc.vector.quantize_mx(out=q_words[:].bitcast(FP8X4), scales=q_plane[:], in_=q_bf[:].rearrange("p q j -> p (q j)"))
+        q_halves = [slice(0, P // 2), slice(P // 2, P)]
+        for cols in q_halves:
+            nc.vector.tensor_copy(
+                out=q_bf[:, cols, :].rearrange("p (c i) j -> p c j i", i=4),
+                in_=q_raw[:, :, cols].rearrange("p j (c i) -> p c j i", i=4),
+            )
+        for cols in q_halves:
+            nc.vector.quantize_mx(
+                out=q_words[:, cols].bitcast(FP8X4), scales=q_plane[:, cols], in_=q_bf[:, cols, :].rearrange("p q j -> p (q j)")
+            )
 
-        def score(name, rhs, rhs_scale, width):
-            bank = psum.tile([P, width], F32, name=name)
+        f1b = sbuf.tile([P, TOKENS], F32, tag="q_bf_then_f1b", align_bytes=64)
+        nc.gpsimd.memset(f1b[:], 0.0)
+
+        def score(name, tag, rhs, rhs_scale, width):
+            bank = psum.tile([P, width], F32, name=name, tag=tag)
             nc.tensor.matmul_mx(
                 out=bank[:], lhsT=q_words[:].bitcast(FP8X4), lhsT_scale=q_plane[:],
                 rhs=rhs, rhs_scale=rhs_scale, start=True, stop=True,
@@ -95,25 +104,35 @@ def tile_attend_scaledhops_three_kernel(
             return bank
 
         a = sbuf.tile([P, TOKENS], F32)
-        piece = 256
-        for k in range(TOKENS // piece):
-            lo = k * piece
+        lo = 0
+        for k, piece in enumerate((256, 256, 256, 128, 128)):
             words = cache_halves[lo // BANK]
-            bank = score("a%d" % k, words[:, lo % BANK : lo % BANK + piece].bitcast(FP8X4), cache_plane[:, lo : lo + piece], piece)
+            bank = score("a%d" % k, "bank%d" % k, words[:, lo % BANK : lo % BANK + piece].bitcast(FP8X4), cache_plane[:, lo : lo + piece], piece)
             if k % 2 == 0:
                 nc.vector.tensor_copy(out=a[:, lo : lo + piece], in_=bank[:])
             else:
                 nc.scalar.activation(out=a[:, lo : lo + piece], in_=bank[:], func=COPY)
+            lo += piece
 
-        w = sbuf.tile([P, SLOTS], F32)
-        nc.scalar.activation(out=w[:], in_=a[:].indirect(idx[:]), func=COPY, scale=sa_col[:])
-        nc.scalar.activation(out=f1[:].indirect(idx2[:]), in_=w[:], func=COPY)
+        share = SLOTS // 2
+        list_halves = [slice(0, LIST_COLS // 2), slice(LIST_COLS // 2, LIST_COLS)]
+        wa = sbuf.tile([P, share], F32)
+        wb = sbuf.tile([P, share], F32)
+        nc.scalar.activation(out=wa[:], in_=a[:].indirect(idx[:, list_halves[0]]), func=COPY, scale=sa_col[:])
+        nc.scalar.activation(out=wb[:], in_=a[:].indirect(idx[:, list_halves[1]]), func=COPY, scale=sa_col[:])
+        nc.scalar.activation(out=f1a[:].indirect(idx2[:, list_halves[0]]), in_=wa[:], func=COPY)
+        nc.scalar.activation(out=f1b[:].indirect(idx2[:, list_halves[1]]), in_=wb[:], func=COPY)
 
-        bb = sbuf.tile([P, TOKENS], F32)
+        f2 = sbuf.tile([P, TOKENS], F32, tag="a_then_f2")
+        nc.vector.memset(f2[:], 0.0)
+
+        part = sbuf.tile([P, TOKENS], F32)
         for half in range(2):
             cols = slice(half * BANK, (half + 1) * BANK)
-            bank = score("b%d" % half, draft[:, 2 * half * BANK : 2 * (half + 1) * BANK].bitcast(FP4X4), draft_plane[:, cols], BANK)
-            nc.vector.tensor_tensor(out=bb[:, cols], in0=bank[:], in1=f1[:, cols], op=SUBTRACT)
+            bank = score("b%d" % half, "bank%d" % (5 + half), draft[:, 2 * half * BANK : 2 * (half + 1) * BANK].bitcast(FP4X4), draft_plane[:, cols], BANK)
+            nc.vector.tensor_tensor(out=part[:, cols], in0=bank[:], in1=f1a[:, cols], op=SUBTRACT)
+        bb = sbuf.tile([P, TOKENS], F32)
+        nc.vector.tensor_tensor(out=bb[:], in0=part[:], in1=f1b[:], op=SUBTRACT)
 
         v = sbuf.tile([P, SLOTS], F32)
         nc.scalar.activation(out=v[:], in_=bb[:].indirect(idx3[:]), func=COPY, scale=sb_col[:])
@@ -122,10 +141,9 @@ def tile_attend_scaledhops_three_kernel(
         cc = sbuf.tile([P, TOKENS], F32)
         for half in range(2):
             cols = slice(half * BANK, (half + 1) * BANK)
-            bank = score("c%d" % half, arch[:, cols].bitcast(FP8X4), arch_plane[:, cols], BANK)
+            bank = score("c%d" % half, "bank%d" % half, arch[:, cols].bitcast(FP8X4), arch_plane[:, cols], BANK)
             nc.vector.tensor_tensor(out=cc[:, cols], in0=bank[:], in1=f2[:, cols], op=MAX)
 
-        share = SLOTS // 2
         y0 = sbuf.tile([P, share], F32)
         y1 = sbuf.tile([P, share], F32)
         nc.vector.tensor_copy(out=y0[:], in_=cc[:].indirect(idx5[:, : LIST_COLS // 2]))

@@ -47,11 +47,13 @@ def tile_attend_scaledhops_three_kernel(
         cache_plane = sbuf.tile([P, TOKENS], U8, align_bytes=64)
         draft_plane = sbuf.tile([P, TOKENS], U8, align_bytes=64)
         arch_plane = sbuf.tile([P, TOKENS], U8, align_bytes=64)
-        f1a = sbuf.tile([P, TOKENS], F32, tag="a_then_f2")
+        f1a = sbuf.tile([P, TOKENS], F32)
         nc.vector.memset(cache_plane[:].bitcast(I32), 0)
         nc.vector.memset(draft_plane[:].bitcast(I32), 0)
         nc.vector.memset(arch_plane[:].bitcast(I32), 0)
         nc.vector.memset(f1a[:], 0.0)
+        f2 = sbuf.tile([P, TOKENS], F32)
+        nc.vector.memset(f2[:], 0.0)
 
         q_raw = sbuf.tile([P, PACK, P], F32)
         nc.sync.dma_start(out=q_raw[:], in_=query.rearrange("(p j) q -> p j q", j=PACK))
@@ -122,9 +124,6 @@ def tile_attend_scaledhops_three_kernel(
         nc.scalar.activation(out=wb[:], in_=a[:].indirect(idx[:, list_halves[1]]), func=COPY, scale=sa_col[:])
         nc.scalar.activation(out=f1a[:].indirect(idx2[:, list_halves[0]]), in_=wa[:], func=COPY)
         nc.scalar.activation(out=f1b[:].indirect(idx2[:, list_halves[1]]), in_=wb[:], func=COPY)
-
-        f2 = sbuf.tile([P, TOKENS], F32, tag="a_then_f2")
-        nc.vector.memset(f2[:], 0.0)
 
         part = sbuf.tile([P, TOKENS], F32)
         for half in range(2):

from contextlib import ExitStack

import concourse.mybir as mybir

F32 = mybir.dt.float32
BF16 = mybir.dt.bfloat16
I32 = mybir.dt.int32
U32 = mybir.dt.uint32
U16 = mybir.dt.uint16
U8 = mybir.dt.uint8
FP8X4 = mybir.dt.float8_e4m3fn_x4
FP4X4 = mybir.dt.float4_e2m1fn_x4
COPY = mybir.ActivationFunctionType.Copy
SUBTRACT = mybir.AluOpType.subtract
MAX = mybir.AluOpType.max

P = 128
PACK = 4
TOKENS = 1024
SLOTS = 512
BANK = 512
LIST_COLS = SLOTS // 16
FLOPS = 3 * 2 * 512 * P * TOKENS


def load_scale_rows(nc, plane, scales):
    rows = scales[0].bitcast(I32)
    for quad in range(4):
        nc.sync.dma_start(out=plane[32 * quad : 32 * quad + 4, :].bitcast(I32), in_=rows[4 * quad : 4 * quad + 4, :])


def load_list(nc, pool, offs, name):
    tile = pool.tile([P, LIST_COLS], U16, name=name)
    nc.sync.dma_start(tile[:], offs)
    return tile


def tile_attend_scaledhops_three_kernel(
    tc, query, cache_words, cache_scales, draft_words, draft_scales, arch_words, arch_scales,
    sa, sb, offs, offs2, offs3, offs4, offs5, out,
):
    nc = tc.nc
    with ExitStack() as ctx:
        sbuf = ctx.enter_context(tc.tile_pool(name="sbuf", bufs=1))
        psum = ctx.enter_context(tc.psum_pool(name="psum", bufs=1))

        cache_plane = sbuf.tile([P, TOKENS], U8, align_bytes=64)
        draft_plane = sbuf.tile([P, TOKENS], U8, align_bytes=64)
        arch_plane = sbuf.tile([P, TOKENS], U8, align_bytes=64)
        f1a = sbuf.tile([P, TOKENS], F32)
        nc.vector.memset(cache_plane[:].bitcast(I32), 0)
        nc.vector.memset(draft_plane[:].bitcast(I32), 0)
        nc.vector.memset(arch_plane[:].bitcast(I32), 0)
        nc.vector.memset(f1a[:], 0.0)
        f2 = sbuf.tile([P, TOKENS], F32)
        nc.vector.memset(f2[:], 0.0)

        q_raw = sbuf.tile([P, PACK, P], F32)
        nc.sync.dma_start(out=q_raw[:], in_=query.rearrange("(p j) q -> p j q", j=PACK))
        load_scale_rows(nc, cache_plane, cache_scales)
        cache_rows = cache_words[0].rearrange("p n t -> p (n t)").bitcast(I32)
        cache_halves = []
        for half in range(2):
            words = sbuf.tile([P, BANK], U32, name="cache%d" % half, align_bytes=64)
            nc.sync.dma_start(out=words[:].bitcast(I32), in_=cache_rows[:, half * BANK : (half + 1) * BANK])
            cache_halves.append(words)
        idx = load_list(nc, sbuf, offs, "idx")
        sa_col = sbuf.tile([P, 1], F32)
        nc.sync.dma_start(out=sa_col[:], in_=sa)
        idx2 = load_list(nc, sbuf, offs2, "idx2")
        load_scale_rows(nc, draft_plane, draft_scales)
        draft = sbuf.tile([P, 2 * TOKENS], U8, align_bytes=64)
        nc.sync.dma_start(out=draft[:].bitcast(I32), in_=draft_words[0].bitcast(I32))
        idx3 = load_list(nc, sbuf, offs3, "idx3")
        sb_col = sbuf.tile([P, 1], F32)
        nc.sync.dma_start(out=sb_col[:], in_=sb)
        idx4 = load_list(nc, sbuf, offs4, "idx4")
        load_scale_rows(nc, arch_plane, arch_scales)
        arch = sbuf.tile([P, TOKENS], U32, align_bytes=64)
        nc.sync.dma_start(out=arch[:].bitcast(I32), in_=arch_words[0].rearrange("p n t -> p (n t)").bitcast(I32))
        idx5 = load_list(nc, sbuf, offs5, "idx5")

        q_bf = sbuf.tile([P, P, PACK], BF16, tag="q_bf_then_f1b", align_bytes=64)
        q_words = sbuf.tile([P, P], U32, align_bytes=64)
        q_plane = sbuf.tile([P, P], U8, align_bytes=64)
        q_halves = [slice(0, P // 2), slice(P // 2, P)]
        for cols in q_halves:
            nc.vector.tensor_copy(
                out=q_bf[:, cols, :].rearrange("p (c i) j -> p c j i", i=4),
                in_=q_raw[:, :, cols].rearrange("p j (c i) -> p c j i", i=4),
            )
        for cols in q_halves:
            nc.vector.quantize_mx(
                out=q_words[:, cols].bitcast(FP8X4), scales=q_plane[:, cols], in_=q_bf[:, cols, :].rearrange("p q j -> p (q j)")
            )

        f1b = sbuf.tile([P, TOKENS], F32, tag="q_bf_then_f1b", align_bytes=64)
        nc.gpsimd.memset(f1b[:], 0.0)

        def score(name, tag, rhs, rhs_scale, width):
            bank = psum.tile([P, width], F32, name=name, tag=tag)
            nc.tensor.matmul_mx(
                out=bank[:], lhsT=q_words[:].bitcast(FP8X4), lhsT_scale=q_plane[:],
                rhs=rhs, rhs_scale=rhs_scale, start=True, stop=True,
            )
            return bank

        a = sbuf.tile([P, TOKENS], F32)
        lo = 0
        for k, piece in enumerate((256, 256, 256, 128, 128)):
            words = cache_halves[lo // BANK]
            bank = score("a%d" % k, "bank%d" % k, words[:, lo % BANK : lo % BANK + piece].bitcast(FP8X4), cache_plane[:, lo : lo + piece], piece)
            if k % 2 == 0:
                nc.vector.tensor_copy(out=a[:, lo : lo + piece], in_=bank[:])
            else:
                nc.scalar.activation(out=a[:, lo : lo + piece], in_=bank[:], func=COPY)
            lo += piece

        share = SLOTS // 2
        list_halves = [slice(0, LIST_COLS // 2), slice(LIST_COLS // 2, LIST_COLS)]
        wa = sbuf.tile([P, share], F32)
        wb = sbuf.tile([P, share], F32)
        nc.scalar.activation(out=wa[:], in_=a[:].indirect(idx[:, list_halves[0]]), func=COPY, scale=sa_col[:])
        nc.scalar.activation(out=wb[:], in_=a[:].indirect(idx[:, list_halves[1]]), func=COPY, scale=sa_col[:])
        nc.scalar.activation(out=f1a[:].indirect(idx2[:, list_halves[0]]), in_=wa[:], func=COPY)
        nc.scalar.activation(out=f1b[:].indirect(idx2[:, list_halves[1]]), in_=wb[:], func=COPY)

        part = sbuf.tile([P, TOKENS], F32)
        for half in range(2):
            cols = slice(half * BANK, (half + 1) * BANK)
            bank = score("b%d" % half, "bank%d" % (5 + half), draft[:, 2 * half * BANK : 2 * (half + 1) * BANK].bitcast(FP4X4), draft_plane[:, cols], BANK)
            nc.vector.tensor_tensor(out=part[:, cols], in0=bank[:], in1=f1a[:, cols], op=SUBTRACT)
        bb = sbuf.tile([P, TOKENS], F32)
        nc.vector.tensor_tensor(out=bb[:], in0=part[:], in1=f1b[:], op=SUBTRACT)

        v = sbuf.tile([P, SLOTS], F32)
        nc.scalar.activation(out=v[:], in_=bb[:].indirect(idx3[:]), func=COPY, scale=sb_col[:])
        nc.scalar.activation(out=f2[:].indirect(idx4[:]), in_=v[:], func=COPY)

        cc = sbuf.tile([P, TOKENS], F32)
        for half in range(2):
            cols = slice(half * BANK, (half + 1) * BANK)
            bank = score("c%d" % half, "bank%d" % half, arch[:, cols].bitcast(FP8X4), arch_plane[:, cols], BANK)
            nc.vector.tensor_tensor(out=cc[:, cols], in0=bank[:], in1=f2[:, cols], op=MAX)

        y0 = sbuf.tile([P, share], F32)
        y1 = sbuf.tile([P, share], F32)
        nc.vector.tensor_copy(out=y0[:], in_=cc[:].indirect(idx5[:, : LIST_COLS // 2]))
        nc.scalar.activation(out=y1[:], in_=cc[:].indirect(idx5[:, LIST_COLS // 2 :]), func=COPY)
        nc.sync.dma_start(out=out[:, :share], in_=y0[:])
        nc.scalar.dma_start(out=out[:, share:], in_=y1[:])
